import numpy as np
import ml_dtypes


def mxq(x, axis, fmt="e4m3"):
    dtype, down = {"e4m3": (ml_dtypes.float8_e4m3fn, 7), "e5m2": (ml_dtypes.float8_e5m2, 14)}[fmt]
    v = np.moveaxis(np.asarray(x, np.float32).astype(ml_dtypes.bfloat16).astype(np.float64), axis, -1)
    blocks = v.reshape(v.shape[:-1] + (-1, 32))
    amax = np.abs(blocks).max(-1, keepdims=True)
    byte = np.maximum(np.where(amax > 0, np.frexp(amax)[1] - 1 + 127, 0) - down, 1)
    scale = np.exp2(byte - 127.0)
    codes = (blocks / scale).astype(np.float32).astype(dtype).astype(np.float64)
    return np.moveaxis((codes * scale).reshape(v.shape), -1, axis)


WIDE = False


def mx_kscale(k):
    if not WIDE:
        return np.ones(k)
    levels = np.array([10, -10, 5, -5, 0])
    if k % 512:
        return np.exp2(np.random.permutation(np.resize(levels, k // 32))).repeat(32)
    a = np.empty((k // 512, 16))
    for p in range(k // 512):
        a[p, :8] = np.random.permutation(np.resize(levels, 8))
        for g in range(8):
            far = levels[np.abs(levels - a[p, g]) >= 10]
            a[p, g + 8] = far[np.random.randint(len(far))]
    return np.exp2(a.ravel()).repeat(32)


def f64(x):
    return np.asarray(x).astype(np.float64)


def striped(idx):
    return np.tile(idx.reshape(-1, 16).T, (8, 1)).astype(np.uint16)


def unstriped(offs):
    return offs[:16].T.reshape(-1).astype(np.int64)


E2M1 = np.array([0.0, 0.5, 1.0, 1.5, 2.0, 3.0, 4.0, 6.0, -0.0, -0.5, -1.0, -1.5, -2.0, -3.0, -4.0, -6.0])


def pack_weight(w, fmt):
    k, n = w.shape
    w = f64(np.asarray(w, np.float32).astype(ml_dtypes.bfloat16)).reshape(k // 32, 32, n)
    amax = np.abs(w).max(1)
    if fmt == "e4m3":
        byte = np.frexp(amax)[1] - 1 + 127 - 7
    else:
        mant, ex = np.frexp(amax / 6.0)
        byte = np.where(mant > 0.5, ex, ex - 1) + 127
    byte = np.clip(np.where(amax > 0, byte, 1), 1, 254)
    scaled = (w * np.exp2(127.0 - byte)[:, None, :]).reshape(k, n).astype(np.float32)
    by_word = np.ascontiguousarray(scaled.reshape(k // 512, 128, 4, n).transpose(0, 1, 3, 2))
    if fmt == "e4m3":
        words = by_word.astype(ml_dtypes.float8_e4m3fn).view(np.uint8)
    else:
        c = by_word.astype(ml_dtypes.float4_e2m1fn).view(np.uint8) & 0xF
        words = (c[..., 0::2] | (c[..., 1::2] << 4)).reshape(k // 512, 128, 2 * n)
    return np.ascontiguousarray(words), np.ascontiguousarray(byte.astype(np.uint8).reshape(k // 512, 16, n))


def unpack_weight(words, scales, fmt):
    g, _, n = scales.shape
    words = np.ascontiguousarray(words).reshape(g, 128, n, -1)
    if fmt == "e4m3":
        vals = words.view(ml_dtypes.float8_e4m3fn).astype(np.float64)
    else:
        nib = np.empty((g, 128, n, 4), np.uint8)
        nib[..., 0::2] = words & 0xF
        nib[..., 1::2] = words >> 4
        vals = E2M1[nib]
    vals = vals * np.repeat(np.exp2(scales.astype(np.float64) - 127.0), 8, axis=1)[..., None]
    return vals.transpose(0, 1, 3, 2).reshape(g * 512, n)


def planes(y):
    n, m = y.shape
    v = y.astype(np.float32).astype(ml_dtypes.bfloat16).astype(np.float64).reshape(n // 32, 32, m)
    top = np.abs(v).max(1)
    byte = np.clip(np.where(top > 0, np.frexp(top)[1] - 1 + 127 - 7, 1), 1, 254)
    codes = (v * np.exp2(127.0 - byte)[:, None, :]).reshape(n, m).astype(np.float32).astype(ml_dtypes.float8_e4m3fn).view(np.uint8)
    words = codes.reshape(n // 512, 128, 4, m).transpose(0, 1, 3, 2)
    return np.ascontiguousarray(words), np.ascontiguousarray(byte.astype(np.uint8).reshape(n // 512, 16, m))


def sigmoid(v):
    return 1.0 / (1.0 + np.exp(-np.maximum(v, -700.0)))


K, T, E, C, H, N = 512, 768, 6, 256, 512, 512


def by_expert(wq, xq):
    return np.concatenate([wq[e].T @ xq[:, e * C:(e + 1) * C] for e in range(E)], axis=1)


def setup_inputs():
    n = np.random.standard_normal
    s = mx_kscale(K)
    u = mx_kscale(H)
    first = np.random.permutation(np.repeat(np.arange(E), T // E))
    second = (first + 1 + np.random.permutation(np.repeat(np.arange(E - 1), -(-T // (E - 1)))[:T])) % E
    while np.bincount(second, minlength=E).max() != T // E:
        load = np.bincount(second, minlength=E); hi, lo = int(load.argmax()), int(load.argmin())
        t = np.flatnonzero((second == hi) & (first != lo))[0]; second[t] = lo
    slot_token = np.empty(E * C, np.int64); pos = np.empty((2, T), np.int64); fill = np.zeros(E, np.int64)
    place = np.stack([np.random.permutation(C) for _ in range(E)])
    for r, deal in enumerate((first, second)):
        for t in np.random.permutation(T):
            e = deal[t]; j = e * C + place[e, fill[e]]; fill[e] += 1; slot_token[j] = t; pos[r, t] = j
    g = np.random.uniform(0.2, 0.8, T)
    x = pack_weight(n((K, T)) * s[:, None], "e4m3")
    w1 = pack_weight(n((K, H)) / np.sqrt(K) / s[:, None], "e2m1")
    w3 = pack_weight(n((K, H)) / np.sqrt(K) / s[:, None] * u, "e2m1")
    w2 = [pack_weight(m, "e2m1") for m in n((E, H, N)) / np.sqrt(H) / u[None, :, None]]
    return {
        "x_words": x[0],
        "x_scales": x[1],
        "w1_words": w1[0],
        "w1_scales": w1[1],
        "w3_words": w3[0],
        "w3_scales": w3[1],
        "w2_words": np.stack([m[0] for m in w2]),
        "w2_scales": np.stack([m[1] for m in w2]),
        "gate": np.stack([np.tile(g, (128, 1)), np.tile(1.0 - g, (128, 1))]).astype(np.float32),
        "offs": striped(slot_token),
        "pos1": striped(pos[0]),
        "pos2": striped(pos[1]),
    }


def reference(x_words, x_scales, w1_words, w1_scales, w3_words, w3_scales, w2_words, w2_scales, gate, offs, pos1, pos2):
    w1 = unpack_weight(w1_words, w1_scales, "e2m1")
    w3 = unpack_weight(w3_words, w3_scales, "e2m1")
    w2 = np.stack([unpack_weight(w2_words[e], w2_scales[e], "e2m1") for e in range(E)])
    idx = unstriped(offs)
    x = unpack_weight(x_words, x_scales, "e4m3")
    h = sigmoid(w1.T @ x) * (w3.T @ x)
    y = by_expert(w2, mxq(h[:, idx], 0, "e4m3"))
    out = sum(f64(gate[r, :1]) * y[:, unstriped(p)] for r, p in enumerate((pos1, pos2)))
    out_0 = out
    return (out_0,) + planes(out_0)

@@ -1,0 +1,192 @@
+from contextlib import ExitStack
+
+import concourse.mybir as mybir
+
+K, T, E, C, H, N = 512, 768, 6, 256, 512, 512
+S = E * C
+FLOPS = 2 * K * H * T * 2 + 2 * H * N * S
+
+F32 = mybir.dt.float32
+BF16 = mybir.dt.bfloat16
+I32 = mybir.dt.int32
+U32 = mybir.dt.uint32
+U16 = mybir.dt.uint16
+U8 = mybir.dt.uint8
+FP8X4 = mybir.dt.float8_e4m3fn_x4
+FP4X4 = mybir.dt.float4_e2m1fn_x4
+MULT = mybir.AluOpType.mult
+ADD = mybir.AluOpType.add
+SIGMOID = mybir.ActivationFunctionType.Sigmoid
+COPY = mybir.ActivationFunctionType.Copy
+
+P = 128
+PACK = 4
+TOK = 256
+SLOT_CHUNKS = ((0, 1), (1, 3), (3, 5), (5, 6))
+TOKEN_CHUNKS = ((0, 512), (512, 768))
+
+
+def tile_moe_sup_glu_sigmoid_kernel(
+    tc, x_words, x_scales, w1_words, w1_scales, w3_words, w3_scales, w2_words, w2_scales, gate, offs, pos1, pos2, out_0, out_1, out_2
+):
+    nc = tc.nc
+    with ExitStack() as ctx:
+        keep = ctx.enter_context(tc.tile_pool(name="keep", bufs=1))
+        ring = ctx.enter_context(tc.tile_pool(name="ring", bufs=2))
+        psum = ctx.enter_context(tc.psum_pool(name="psum", bufs=8))
+
+        offs_sb = keep.tile([P, S // 16], U16, name="offs_sb")
+        pos1_sb = keep.tile([P, T // 16], U16, name="pos1_sb")
+        pos2_sb = keep.tile([P, T // 16], U16, name="pos2_sb")
+
+        x_codes = keep.tile([P, T], U32, name="x_codes", align_bytes=64)
+        x_plane = keep.tile([P, T], U8, name="x_plane", align_bytes=64)
+        first_raw = [keep.tile([P, 2 * H], U8, name=f"first_raw{m}") for m in range(2)]
+        first_raw_plane = [keep.tile([P, H], U8, name=f"first_raw_plane{m}") for m in range(2)]
+        first_codes = [keep.tile([P, 2 * H], U8, name=f"first_codes{m}", align_bytes=64) for m in range(2)]
+        first_plane = [keep.tile([P, H], U8, name=f"first_plane{m}", align_bytes=64) for m in range(2)]
+        w2_raw = [keep.tile([P, e1 - e0, 2 * N], U8, name=f"w2_raw{e0}") for e0, e1 in SLOT_CHUNKS]
+        w2_raw_plane = keep.tile([P, E, N], U8, name="w2_raw_plane")
+        w2_plane = [keep.tile([P, N], U8, name=f"w2_plane{e}", align_bytes=64) for e in range(E)]
+        gates = [keep.tile([P, T], F32, name=f"gate{r}") for r in range(2)]
+
+        def load_scale_rows(plane, rows):
+            for r in range(4):
+                nc.sync.dma_start(out=plane[r:P:32].bitcast(I32), in_=rows[r:16:4].bitcast(I32))
+
+        def deal_words(engine_copy, dst, src):
+            engine_copy(
+                out=dst.bitcast(U16).rearrange("p (t b i) -> p b t i", t=PACK, i=8),
+                in_=src.bitcast(U16).rearrange("p (b i t) -> p b t i", t=PACK, i=8),
+            )
+
+        def deal_bytes(engine_copy, dst, src):
+            engine_copy(
+                out=dst.rearrange("p (t b i) -> p b t i", t=PACK, i=16),
+                in_=src.rearrange("p (b i t) -> p b t i", t=PACK, i=16),
+            )
+
+        nc.vector.memset(first_raw_plane[0][:].bitcast(I32), 0)
+        nc.vector.memset(x_plane[:].bitcast(I32), 0)
+        nc.vector.memset(first_raw_plane[1][:].bitcast(I32), 0)
+        nc.gpsimd.memset(w2_raw_plane[:].rearrange("p e n -> p (e n)").bitcast(I32), 0)
+
+        nc.sync.dma_start(out=first_raw[0][:].bitcast(I32), in_=w1_words[0].bitcast(I32))
+        load_scale_rows(first_raw_plane[0], w1_scales[0])
+        nc.sync.dma_start(out=x_codes[:].bitcast(I32), in_=x_words[0].rearrange("p n t -> p (n t)").bitcast(I32))
+        load_scale_rows(x_plane, x_scales[0])
+        nc.sync.dma_start(out=first_raw[1][:].bitcast(I32), in_=w3_words[0].bitcast(I32))
+        load_scale_rows(first_raw_plane[1], w3_scales[0])
+        nc.sync.dma_start(offs_sb[:], offs)
+        load_scale_rows(w2_raw_plane, w2_scales[:, 0].rearrange("e q n -> q e n"))
+        for c, (e0, e1) in enumerate(SLOT_CHUNKS):
+            nc.sync.dma_start(out=w2_raw[c][:].bitcast(I32), in_=w2_words[e0:e1, 0].rearrange("e p b -> p e b").bitcast(I32))
+        nc.sync.dma_start(pos1_sb[:], pos1)
+        nc.sync.dma_start(pos2_sb[:], pos2)
+        for r in range(2):
+            nc.sync.dma_start(out=gates[r][:], in_=gate[r])
+
+        for m in range(2):
+            deal_words(nc.vector.tensor_copy, first_codes[m][:], first_raw[m][:])
+            deal_bytes(nc.vector.tensor_copy, first_plane[m][:], first_raw_plane[m][:])
+
+        h_pairs = [keep.tile([P, T], U32, name=f"h_pairs{u}") for u in range(2)]
+        for u in range(2):
+            for t0 in range(0, T, TOK):
+                cols = slice(t0, t0 + TOK)
+                sums = []
+                for m in range(2):
+                    bank = psum.tile([P, 2, TOK], F32, name="bank", tag="bank")
+                    for j in range(2):
+                        t = 2 * u + j
+                        nc.tensor.matmul_mx(
+                            out=bank[:, j, :],
+                            lhsT=first_codes[m][:, 2 * P * t : 2 * P * (t + 1)].bitcast(FP4X4),
+                            lhsT_scale=first_plane[m][:, P * t : P * (t + 1)],
+                            rhs=x_codes[:, cols].bitcast(FP8X4),
+                            rhs_scale=x_plane[:, cols],
+                            start=True,
+                            stop=True,
+                        )
+                    sums.append(bank)
+                sig = keep.tile([P, TOK, 2], F32, name="sig", tag=f"shared{t0}", align_bytes=64)
+                nc.scalar.activation(out=sig[:], in_=sums[0][:].rearrange("p j n -> p n j"), func=SIGMOID)
+                nc.vector.tensor_tensor(
+                    out=h_pairs[u][:, cols].bitcast(BF16).rearrange("p (n j) -> p n j", j=2),
+                    in0=sums[1][:].rearrange("p j n -> p n j"),
+                    in1=sig[:],
+                    op=MULT,
+                )
+
+        w2_pairs = [keep.tile([P, 2, 2 * N], U8, name="w2_pair", tag=f"shared{t0}", align_bytes=64) for t0 in range(0, T, TOK)]
+        w2_codes = [w2_pairs[e // 2][:, e % 2, :] for e in range(E)]
+        for c, (e0, e1) in enumerate(SLOT_CHUNKS):
+            for e in range(e0, e1):
+                deal_bytes(nc.gpsimd.tensor_copy, w2_plane[e][:], w2_raw_plane[:, e, :])
+                deal_words(nc.scalar.copy, w2_codes[e], w2_raw[c][:, e - e0, :])
+
+        y = [keep.tile([P, S], F32, name=f"y{t}") for t in range(PACK)]
+        for e0, e1 in SLOT_CHUNKS:
+            n = (e1 - e0) * C
+            picked = ring.tile([P, 2, n], U32, name="picked")
+            for u in range(2):
+                nc.vector.tensor_copy(out=picked[:, u, :], in_=h_pairs[u][:].indirect(offs_sb[:, e0 * C // 16 : e1 * C // 16]))
+            woven = ring.tile([P, n, 2], U32, name="woven", align_bytes=64)
+            nc.gpsimd.tensor_copy(out=woven[:], in_=picked[:].rearrange("p u n -> p n u"))
+            h_codes = ring.tile([P, n], U32, name="h_codes", align_bytes=64)
+            h_plane = ring.tile([P, n], U8, name="h_plane", align_bytes=64)
+            nc.vector.quantize_mx(
+                out=h_codes[:].bitcast(FP8X4), scales=h_plane[:], in_=woven[:].rearrange("p n u -> p (n u)").bitcast(BF16)
+            )
+            for t in range(PACK):
+                bank = psum.tile([P, n], F32, name="bank", tag="bank")
+                for e in range(e0, e1):
+                    cols = slice((e - e0) * C, (e - e0 + 1) * C)
+                    nc.tensor.matmul_mx(
+                        out=bank[:, cols],
+                        lhsT=w2_codes[e][:, 2 * P * t : 2 * P * (t + 1)].bitcast(FP4X4),
+                        lhsT_scale=w2_plane[e][:, P * t : P * (t + 1)],
+                        rhs=h_codes[:, cols].bitcast(FP8X4),
+                        rhs_scale=h_plane[:, cols],
+                        start=True,
+                        stop=True,
+                    )
+                if e1 == E and t % 2 == 0:
+                    nc.vector.tensor_copy(out=y[t][:, e0 * C : e1 * C], in_=bank[:])
+                else:
+                    nc.scalar.copy(out=y[t][:, e0 * C : e1 * C], in_=bank[:])
+
+        out_codes = keep.tile([P, T], U32, name="out_codes", align_bytes=64)
+        out_plane = keep.tile([P, T], U8, name="out_plane", align_bytes=64)
+        out_rows = out_0.rearrange("(p t) c -> p t c", t=PACK)
+        for t0, t1 in TOKEN_CHUNKS:
+            n = t1 - t0
+            lists = slice(t0 // 16, t1 // 16)
+            first = keep.tile([P, PACK, n], F32, name=f"first{t0}")
+            second = keep.tile([P, PACK, n], F32, name=f"second{t0}")
+            total = keep.tile([P, PACK, n], F32, name=f"total{t0}")
+            for t in range(PACK):
+                nc.scalar.activation(out=second[:, t, :], in_=y[t][:].indirect(pos2_sb[:, lists]), func=COPY)
+                if t < PACK - 1:
+                    nc.vector.tensor_tensor(out=first[:, t, :], in0=y[t][:].indirect(pos1_sb[:, lists]), in1=gates[0][:, t0:t1], op=MULT)
+                else:
+                    nc.scalar.activation(out=first[:, t, :], in_=y[t][:].indirect(pos1_sb[:, lists]), func=COPY)
+                    nc.vector.tensor_tensor(out=first[:, t, :], in0=first[:, t, :], in1=gates[0][:, t0:t1], op=MULT)
+                nc.vector.tensor_tensor(out=second[:, t, :], in0=second[:, t, :], in1=gates[1][:, t0:t1], op=MULT)
+                nc.vector.tensor_tensor(out=total[:, t, :], in0=first[:, t, :], in1=second[:, t, :], op=ADD)
+                nc.sync.dma_start(out=out_rows[:, t, t0:t1], in_=total[:, t, :])
+            rounded = keep.tile([P, n, PACK], BF16, name=f"rounded{t0}", align_bytes=64)
+            round_copy = nc.scalar.copy if t1 < T else nc.vector.tensor_copy
+            round_copy(
+                out=rounded[:].rearrange("p (c i) t -> p c t i", i=4),
+                in_=total[:].rearrange("p t (c i) -> p c t i", i=4),
+            )
+            nc.vector.quantize_mx(
+                out=out_codes[:, t0:t1].bitcast(FP8X4), scales=out_plane[:, t0:t1], in_=rounded[:].rearrange("p c t -> p (c t)")
+            )
+            nc.sync.dma_start(
+                out=out_1[0, :, t0:t1, :].rearrange("p c d -> p (c d)").bitcast(I32), in_=out_codes[:, t0:t1].bitcast(I32)
+            )
+        for r in range(4):
+            queue = nc.sync if r % 2 == 0 else nc.scalar
+            queue.dma_start(out=out_2[0, r:16:4].bitcast(I32), in_=out_plane[r:P:32].bitcast(I32))

@@ -1,6 +1,7 @@
 from contextlib import ExitStack
 
 import concourse.mybir as mybir
+from concourse.masks import make_identity
 
 K, T, E, C, H, N = 512, 768, 6, 256, 512, 512
 S = E * C
@@ -22,8 +23,8 @@ COPY = mybir.ActivationFunctionType.Copy
 P = 128
 PACK = 4
 TOK = 256
-SLOT_CHUNKS = ((0, 1), (1, 3), (3, 5), (5, 6))
-TOKEN_CHUNKS = ((0, 512), (512, 768))
+SLOT_CHUNKS = tuple((e, e + 1) for e in range(E))
+TOKEN_CHUNKS = ((0, 256), (256, 512), (512, 768))
 
 
 def tile_moe_sup_glu_sigmoid_kernel(
@@ -33,7 +34,7 @@ def tile_moe_sup_glu_sigmoid_kernel(
     with ExitStack() as ctx:
         keep = ctx.enter_context(tc.tile_pool(name="keep", bufs=1))
         ring = ctx.enter_context(tc.tile_pool(name="ring", bufs=2))
-        psum = ctx.enter_context(tc.psum_pool(name="psum", bufs=8))
+        psum = ctx.enter_context(tc.psum_pool(name="psum", bufs=5))
 
         offs_sb = keep.tile([P, S // 16], U16, name="offs_sb")
         pos1_sb = keep.tile([P, T // 16], U16, name="pos1_sb")
@@ -48,10 +49,11 @@ def tile_moe_sup_glu_sigmoid_kernel(
         w2_raw = [keep.tile([P, e1 - e0, 2 * N], U8, name=f"w2_raw{e0}") for e0, e1 in SLOT_CHUNKS]
         w2_raw_plane = keep.tile([P, E, N], U8, name="w2_raw_plane")
         w2_plane = [keep.tile([P, N], U8, name=f"w2_plane{e}", align_bytes=64) for e in range(E)]
-        gates = [keep.tile([P, T], F32, name=f"gate{r}") for r in range(2)]
+        gate_cols = [keep.tile([P, T // P], F32, name=f"gate_cols{r}") for r in range(2)]
+        identity = keep.tile([P, P], F32, name="identity")
 
-        def load_scale_rows(plane, rows):
-            for r in range(4):
+        def load_scale_rows(plane, rows, which):
+            for r in which:
                 nc.sync.dma_start(out=plane[r:P:32].bitcast(I32), in_=rows[r:16:4].bitcast(I32))
 
         def deal_words(engine_copy, dst, src):
@@ -72,19 +74,22 @@ def tile_moe_sup_glu_sigmoid_kernel(
         nc.gpsimd.memset(w2_raw_plane[:].rearrange("p e n -> p (e n)").bitcast(I32), 0)
 
         nc.sync.dma_start(out=first_raw[0][:].bitcast(I32), in_=w1_words[0].bitcast(I32))
-        load_scale_rows(first_raw_plane[0], w1_scales[0])
-        nc.sync.dma_start(out=x_codes[:].bitcast(I32), in_=x_words[0].rearrange("p n t -> p (n t)").bitcast(I32))
-        load_scale_rows(x_plane, x_scales[0])
+        load_scale_rows(first_raw_plane[0], w1_scales[0], range(4))
         nc.sync.dma_start(out=first_raw[1][:].bitcast(I32), in_=w3_words[0].bitcast(I32))
-        load_scale_rows(first_raw_plane[1], w3_scales[0])
+        load_scale_rows(x_plane, x_scales[0], range(1))
+        nc.sync.dma_start(out=x_codes[:].bitcast(I32), in_=x_words[0].rearrange("p n t -> p (n t)").bitcast(I32))
+        load_scale_rows(x_plane, x_scales[0], range(1, 4))
+        load_scale_rows(first_raw_plane[1], w3_scales[0], range(4))
         nc.sync.dma_start(offs_sb[:], offs)
-        load_scale_rows(w2_raw_plane, w2_scales[:, 0].rearrange("e q n -> q e n"))
+        load_scale_rows(w2_raw_plane, w2_scales[:, 0].rearrange("e q n -> q e n"), range(4))
         for c, (e0, e1) in enumerate(SLOT_CHUNKS):
             nc.sync.dma_start(out=w2_raw[c][:].bitcast(I32), in_=w2_words[e0:e1, 0].rearrange("e p b -> p e b").bitcast(I32))
         nc.sync.dma_start(pos1_sb[:], pos1)
         nc.sync.dma_start(pos2_sb[:], pos2)
         for r in range(2):
-            nc.sync.dma_start(out=gates[r][:], in_=gate[r])
+            with nc.allow_non_contiguous_dma(reason="one weight a partition"):
+                nc.sync.dma_start(out=gate_cols[r][:], in_=gate[r, 0].rearrange("(b c) -> c b", c=P))
+        make_identity(nc, identity[:])
 
         for m in range(2):
             deal_words(nc.vector.tensor_copy, first_codes[m][:], first_raw[m][:])
@@ -125,21 +130,29 @@ def tile_moe_sup_glu_sigmoid_kernel(
                 deal_bytes(nc.gpsimd.tensor_copy, w2_plane[e][:], w2_raw_plane[:, e, :])
                 deal_words(nc.scalar.copy, w2_codes[e], w2_raw[c][:, e - e0, :])
 
+        gate_banks = [psum.tile([P, 2, TOK], F32, name=f"gate_bank{j}", bufs=1) for j in range(T // TOK)]
+        for b in range(T // P):
+            for r in range(2):
+                nc.tensor.transpose(
+                    gate_banks[b // 2][:, r, b % 2 * P : (b % 2 + 1) * P], gate_cols[r][:, b : b + 1].to_broadcast([P, P]), identity[:]
+                )
+
         y = [keep.tile([P, S], F32, name=f"y{t}") for t in range(PACK)]
-        for e0, e1 in SLOT_CHUNKS:
+        for c, (e0, e1) in enumerate(SLOT_CHUNKS):
             n = (e1 - e0) * C
-            picked = ring.tile([P, 2, n], U32, name="picked")
+            picked = keep.tile([P, 2, n], U32, name="picked", tag=f"stage{c % 2}{c // 2 % 2}", align_bytes=64)
             for u in range(2):
                 nc.vector.tensor_copy(out=picked[:, u, :], in_=h_pairs[u][:].indirect(offs_sb[:, e0 * C // 16 : e1 * C // 16]))
-            woven = ring.tile([P, n, 2], U32, name="woven", align_bytes=64)
+            woven = keep.tile([P, n, 2], U32, name="woven", tag=f"stage{c % 2}{1 - c // 2 % 2}", align_bytes=64)
             nc.gpsimd.tensor_copy(out=woven[:], in_=picked[:].rearrange("p u n -> p n u"))
             h_codes = ring.tile([P, n], U32, name="h_codes", align_bytes=64)
             h_plane = ring.tile([P, n], U8, name="h_plane", align_bytes=64)
             nc.vector.quantize_mx(
                 out=h_codes[:].bitcast(FP8X4), scales=h_plane[:], in_=woven[:].rearrange("p n u -> p (n u)").bitcast(BF16)
             )
+            banks = [psum.tile([P, 2, n], F32, name="bank", tag="bank") for u in range(2)]
             for t in range(PACK):
-                bank = psum.tile([P, n], F32, name="bank", tag="bank")
+                bank = banks[t // 2][:, t % 2, :]
                 for e in range(e0, e1):
                     cols = slice((e - e0) * C, (e - e0 + 1) * C)
                     nc.tensor.matmul_mx(
@@ -151,7 +164,9 @@ def tile_moe_sup_glu_sigmoid_kernel(
                         start=True,
                         stop=True,
                     )
-                if e1 == E and t % 2 == 0:
+            for t in range(PACK):
+                bank = banks[t // 2][:, t % 2, :]
+                if e1 == E and t < 2:
                     nc.vector.tensor_copy(out=y[t][:, e0 * C : e1 * C], in_=bank[:])
                 else:
                     nc.scalar.copy(out=y[t][:, e0 * C : e1 * C], in_=bank[:])
@@ -159,28 +174,31 @@ def tile_moe_sup_glu_sigmoid_kernel(
         out_codes = keep.tile([P, T], U32, name="out_codes", align_bytes=64)
         out_plane = keep.tile([P, T], U8, name="out_plane", align_bytes=64)
         out_rows = out_0.rearrange("(p t) c -> p t c", t=PACK)
-        for t0, t1 in TOKEN_CHUNKS:
+        for c, (t0, t1) in enumerate(TOKEN_CHUNKS):
             n = t1 - t0
             lists = slice(t0 // 16, t1 // 16)
-            first = keep.tile([P, PACK, n], F32, name=f"first{t0}")
-            second = keep.tile([P, PACK, n], F32, name=f"second{t0}")
+            last = t1 == T
+            weights = gate_banks[t0 // TOK][:, :, t0 % TOK : t0 % TOK + n]
             total = keep.tile([P, PACK, n], F32, name=f"total{t0}")
-            for t in range(PACK):
-                nc.scalar.activation(out=second[:, t, :], in_=y[t][:].indirect(pos2_sb[:, lists]), func=COPY)
-                if t < PACK - 1:
-                    nc.vector.tensor_tensor(out=first[:, t, :], in0=y[t][:].indirect(pos1_sb[:, lists]), in1=gates[0][:, t0:t1], op=MULT)
-                else:
-                    nc.scalar.activation(out=first[:, t, :], in_=y[t][:].indirect(pos1_sb[:, lists]), func=COPY)
-                    nc.vector.tensor_tensor(out=first[:, t, :], in0=first[:, t, :], in1=gates[0][:, t0:t1], op=MULT)
-                nc.vector.tensor_tensor(out=second[:, t, :], in0=second[:, t, :], in1=gates[1][:, t0:t1], op=MULT)
-                nc.vector.tensor_tensor(out=total[:, t, :], in0=first[:, t, :], in1=second[:, t, :], op=ADD)
-                nc.sync.dma_start(out=out_rows[:, t, t0:t1], in_=total[:, t, :])
             rounded = keep.tile([P, n, PACK], BF16, name=f"rounded{t0}", align_bytes=64)
-            round_copy = nc.scalar.copy if t1 < T else nc.vector.tensor_copy
-            round_copy(
-                out=rounded[:].rearrange("p (c i) t -> p c t i", i=4),
-                in_=total[:].rearrange("p t (c i) -> p c t i", i=4),
-            )
+            for t in range(PACK):
+                terms = ring.tile([P, 2, n], F32, name="terms", bufs=4)
+                for r, pos_sb in enumerate((pos1_sb, pos2_sb)):
+                    looked_up = y[t][:].indirect(pos_sb[:, lists])
+                    if r == 0 and (t % 2 == 0 or t0 == 0 and t == 1):
+                        nc.vector.tensor_copy(out=terms[:, r, :], in_=looked_up)
+                    else:
+                        nc.scalar.activation(out=terms[:, r, :], in_=looked_up, func=COPY)
+                nc.vector.tensor_tensor(out=terms[:], in0=terms[:], in1=weights, op=MULT)
+                adder = nc.vector if last and t >= 2 else nc.gpsimd
+                adder.tensor_tensor(out=total[:, t, :], in0=terms[:, 0, :], in1=terms[:, 1, :], op=ADD)
+                nc.sync.dma_start(out=out_rows[:, t, t0:t1], in_=total[:, t, :])
+            if last:
+                nc.vector.tensor_copy(
+                    out=rounded[:].rearrange("p (c i) t -> p c t i", i=4), in_=total[:].rearrange("p t (c i) -> p c t i", i=4)
+                )
+            else:
+                nc.gpsimd.tensor_copy(out=rounded[:], in_=total[:].rearrange("p t c -> p c t"))
             nc.vector.quantize_mx(
                 out=out_codes[:, t0:t1].bitcast(FP8X4), scales=out_plane[:, t0:t1], in_=rounded[:].rearrange("p c t -> p (c t)")
             )

@@ -1,7 +1,6 @@
 from contextlib import ExitStack
 
 import concourse.mybir as mybir
-from concourse.masks import make_identity
 
 K, T, E, C, H, N = 512, 768, 6, 256, 512, 512
 S = E * C
@@ -23,8 +22,7 @@ COPY = mybir.ActivationFunctionType.Copy
 P = 128
 PACK = 4
 TOK = 256
-SLOT_CHUNKS = tuple((e, e + 1) for e in range(E))
-TOKEN_CHUNKS = ((0, 256), (256, 512), (512, 768))
+TOKEN_CHUNKS = ((0, 512), (512, 768))
 
 
 def tile_moe_sup_glu_sigmoid_kernel(
@@ -34,7 +32,7 @@ def tile_moe_sup_glu_sigmoid_kernel(
     with ExitStack() as ctx:
         keep = ctx.enter_context(tc.tile_pool(name="keep", bufs=1))
         ring = ctx.enter_context(tc.tile_pool(name="ring", bufs=2))
-        psum = ctx.enter_context(tc.psum_pool(name="psum", bufs=5))
+        psum = ctx.enter_context(tc.psum_pool(name="psum", bufs=8))
 
         offs_sb = keep.tile([P, S // 16], U16, name="offs_sb")
         pos1_sb = keep.tile([P, T // 16], U16, name="pos1_sb")
@@ -46,11 +44,12 @@ def tile_moe_sup_glu_sigmoid_kernel(
         first_raw_plane = [keep.tile([P, H], U8, name=f"first_raw_plane{m}") for m in range(2)]
         first_codes = [keep.tile([P, 2 * H], U8, name=f"first_codes{m}", align_bytes=64) for m in range(2)]
         first_plane = [keep.tile([P, H], U8, name=f"first_plane{m}", align_bytes=64) for m in range(2)]
-        w2_raw = [keep.tile([P, e1 - e0, 2 * N], U8, name=f"w2_raw{e0}") for e0, e1 in SLOT_CHUNKS]
-        w2_raw_plane = keep.tile([P, E, N], U8, name="w2_raw_plane")
-        w2_plane = [keep.tile([P, N], U8, name=f"w2_plane{e}", align_bytes=64) for e in range(E)]
-        gate_cols = [keep.tile([P, T // P], F32, name=f"gate_cols{r}") for r in range(2)]
-        identity = keep.tile([P, P], F32, name="identity")
+        w2_raw = [keep.tile([P, 2, 2 * N], U8, name=f"w2_raw{c}") for c in range(E // 2)]
+        w2_raw_plane = keep.tile([P, 2, N], U8, name="w2_raw_plane")
+        w2_dealt_plane = keep.tile([P, 2, N], U8, name="w2_dealt_plane", align_bytes=64)
+        w2_moved_plane = keep.tile([P, 4, N], U8, name="w2_moved_plane", align_bytes=64)
+        w2_plane = [w2_dealt_plane[:, e // 4, :] if e % 4 == 0 else w2_moved_plane[:, e - 1 - e // 4, :] for e in range(E)]
+        gates = keep.tile([P, 2, T], F32, name="gates")
 
         def load_scale_rows(plane, rows, which):
             for r in which:
@@ -68,10 +67,11 @@ def tile_moe_sup_glu_sigmoid_kernel(
                 in_=src.rearrange("p (b i t) -> p b t i", t=PACK, i=16),
             )
 
-        nc.vector.memset(first_raw_plane[0][:].bitcast(I32), 0)
-        nc.vector.memset(x_plane[:].bitcast(I32), 0)
-        nc.vector.memset(first_raw_plane[1][:].bitcast(I32), 0)
+        nc.gpsimd.memset(first_raw_plane[0][:].bitcast(I32), 0)
+        nc.gpsimd.memset(x_plane[:].bitcast(I32), 0)
+        nc.gpsimd.memset(first_raw_plane[1][:].bitcast(I32), 0)
         nc.gpsimd.memset(w2_raw_plane[:].rearrange("p e n -> p (e n)").bitcast(I32), 0)
+        nc.gpsimd.memset(w2_moved_plane[:].rearrange("p e n -> p (e n)").bitcast(I32), 0)
 
         nc.sync.dma_start(out=first_raw[0][:].bitcast(I32), in_=w1_words[0].bitcast(I32))
         load_scale_rows(first_raw_plane[0], w1_scales[0], range(4))
@@ -81,15 +81,17 @@ def tile_moe_sup_glu_sigmoid_kernel(
         load_scale_rows(x_plane, x_scales[0], range(1, 4))
         load_scale_rows(first_raw_plane[1], w3_scales[0], range(4))
         nc.sync.dma_start(offs_sb[:], offs)
-        load_scale_rows(w2_raw_plane, w2_scales[:, 0].rearrange("e q n -> q e n"), range(4))
-        for c, (e0, e1) in enumerate(SLOT_CHUNKS):
-            nc.sync.dma_start(out=w2_raw[c][:].bitcast(I32), in_=w2_words[e0:e1, 0].rearrange("e p b -> p e b").bitcast(I32))
+        for g, (e0, e1) in enumerate(((0, 4), (4, E))):
+            for q in range(4):
+                nc.sync.dma_start(
+                    out=w2_raw_plane[32 * q : 32 * q + 4 * (e1 - e0), g, :].bitcast(I32),
+                    in_=w2_scales[e0:e1, 0, 4 * q : 4 * q + 4, :].bitcast(I32),
+                )
+        for c in range(E // 2):
+            nc.sync.dma_start(out=w2_raw[c][:].bitcast(I32), in_=w2_words[2 * c : 2 * c + 2, 0].rearrange("e p b -> p e b").bitcast(I32))
         nc.sync.dma_start(pos1_sb[:], pos1)
         nc.sync.dma_start(pos2_sb[:], pos2)
-        for r in range(2):
-            with nc.allow_non_contiguous_dma(reason="one weight a partition"):
-                nc.sync.dma_start(out=gate_cols[r][:], in_=gate[r, 0].rearrange("(b c) -> c b", c=P))
-        make_identity(nc, identity[:])
+        nc.sync.dma_start(out=gates[:], in_=gate.rearrange("r p c -> p r c"))
 
         for m in range(2):
             deal_words(nc.vector.tensor_copy, first_codes[m][:], first_raw[m][:])
@@ -125,80 +127,90 @@ def tile_moe_sup_glu_sigmoid_kernel(
 
         w2_pairs = [keep.tile([P, 2, 2 * N], U8, name="w2_pair", tag=f"shared{t0}", align_bytes=64) for t0 in range(0, T, TOK)]
         w2_codes = [w2_pairs[e // 2][:, e % 2, :] for e in range(E)]
-        for c, (e0, e1) in enumerate(SLOT_CHUNKS):
-            for e in range(e0, e1):
-                deal_bytes(nc.gpsimd.tensor_copy, w2_plane[e][:], w2_raw_plane[:, e, :])
-                deal_words(nc.scalar.copy, w2_codes[e], w2_raw[c][:, e - e0, :])
-
-        gate_banks = [psum.tile([P, 2, TOK], F32, name=f"gate_bank{j}", bufs=1) for j in range(T // TOK)]
-        for b in range(T // P):
-            for r in range(2):
-                nc.tensor.transpose(
-                    gate_banks[b // 2][:, r, b % 2 * P : (b % 2 + 1) * P], gate_cols[r][:, b : b + 1].to_broadcast([P, P]), identity[:]
-                )
+        for g in range(2):
+            deal_bytes(nc.vector.tensor_copy, w2_dealt_plane[:, g, :], w2_raw_plane[:, g, :])
+        for e in range(E):
+            if e % 4:
+                for r in range(4):
+                    nc.sync.dma_start(
+                        out=w2_plane[e][r:P:32].bitcast(I32), in_=w2_dealt_plane[4 * (e % 4) + r : P : 32, e // 4, :].bitcast(I32)
+                    )
 
         y = [keep.tile([P, S], F32, name=f"y{t}") for t in range(PACK)]
-        for c, (e0, e1) in enumerate(SLOT_CHUNKS):
-            n = (e1 - e0) * C
-            picked = keep.tile([P, 2, n], U32, name="picked", tag=f"stage{c % 2}{c // 2 % 2}", align_bytes=64)
-            for u in range(2):
-                nc.vector.tensor_copy(out=picked[:, u, :], in_=h_pairs[u][:].indirect(offs_sb[:, e0 * C // 16 : e1 * C // 16]))
-            woven = keep.tile([P, n, 2], U32, name="woven", tag=f"stage{c % 2}{1 - c // 2 % 2}", align_bytes=64)
-            nc.gpsimd.tensor_copy(out=woven[:], in_=picked[:].rearrange("p u n -> p n u"))
-            h_codes = ring.tile([P, n], U32, name="h_codes", align_bytes=64)
-            h_plane = ring.tile([P, n], U8, name="h_plane", align_bytes=64)
+        picked, woven = {}, {}
+
+        def pick(e, u):
+            if u == 0:
+                picked[e] = keep.tile([P, 2, C], U32, name="picked", tag=f"stage{e % 2}{e // 2 % 2}", align_bytes=64)
+            nc.vector.tensor_copy(out=picked[e][:, u, :], in_=h_pairs[u][:].indirect(offs_sb[:, e * C // 16 : (e + 1) * C // 16]))
+
+        def weave(e):
+            woven[e] = keep.tile([P, C, 2], U32, name="woven", tag=f"stage{e % 2}{1 - e // 2 % 2}", align_bytes=64)
+            if False:
+                nc.scalar.copy(out=woven[e][:], in_=picked[e][:].rearrange("p u n -> p n u"))
+            else:
+                nc.vector.tensor_copy(out=woven[e][:].bitcast(I32), in_=picked[e][:].bitcast(I32).rearrange("p u n -> p n u"))
+
+        def expert(e):
+            deal_words(nc.scalar.copy, w2_codes[e], w2_raw[e // 2][:, e % 2, :])
+            h_codes = ring.tile([P, C], U32, name="h_codes", align_bytes=64)
+            h_plane = ring.tile([P, C], U8, name="h_plane", align_bytes=64)
             nc.vector.quantize_mx(
-                out=h_codes[:].bitcast(FP8X4), scales=h_plane[:], in_=woven[:].rearrange("p n u -> p (n u)").bitcast(BF16)
+                out=h_codes[:].bitcast(FP8X4), scales=h_plane[:], in_=woven[e][:].rearrange("p n u -> p (n u)").bitcast(BF16)
             )
-            banks = [psum.tile([P, 2, n], F32, name="bank", tag="bank") for u in range(2)]
             for t in range(PACK):
-                bank = banks[t // 2][:, t % 2, :]
-                for e in range(e0, e1):
-                    cols = slice((e - e0) * C, (e - e0 + 1) * C)
-                    nc.tensor.matmul_mx(
-                        out=bank[:, cols],
-                        lhsT=w2_codes[e][:, 2 * P * t : 2 * P * (t + 1)].bitcast(FP4X4),
-                        lhsT_scale=w2_plane[e][:, P * t : P * (t + 1)],
-                        rhs=h_codes[:, cols].bitcast(FP8X4),
-                        rhs_scale=h_plane[:, cols],
-                        start=True,
-                        stop=True,
-                    )
-            for t in range(PACK):
-                bank = banks[t // 2][:, t % 2, :]
-                if e1 == E and t < 2:
-                    nc.vector.tensor_copy(out=y[t][:, e0 * C : e1 * C], in_=bank[:])
+                bank = psum.tile([P, C], F32, name="bank", tag="bank")
+                nc.tensor.matmul_mx(
+                    out=bank[:],
+                    lhsT=w2_codes[e][:, 2 * P * t : 2 * P * (t + 1)].bitcast(FP4X4),
+                    lhsT_scale=w2_plane[e][:, P * t : P * (t + 1)],
+                    rhs=h_codes[:].bitcast(FP8X4),
+                    rhs_scale=h_plane[:],
+                    start=True,
+                    stop=True,
+                )
+                if e == E - 1 and t >= 2:
+                    nc.vector.tensor_copy(out=y[t][:, e * C : (e + 1) * C], in_=bank[:])
                 else:
-                    nc.scalar.copy(out=y[t][:, e0 * C : e1 * C], in_=bank[:])
+                    nc.scalar.copy(out=y[t][:, e * C : (e + 1) * C], in_=bank[:])
+
+        pick(0, 0)
+        pick(0, 1)
+        for e in range(E):
+            if e + 1 < E:
+                pick(e + 1, 0)
+            weave(e)
+            if e + 1 < E:
+                pick(e + 1, 1)
+            expert(e)
 
         out_codes = keep.tile([P, T], U32, name="out_codes", align_bytes=64)
         out_plane = keep.tile([P, T], U8, name="out_plane", align_bytes=64)
         out_rows = out_0.rearrange("(p t) c -> p t c", t=PACK)
         for c, (t0, t1) in enumerate(TOKEN_CHUNKS):
             n = t1 - t0
-            lists = slice(t0 // 16, t1 // 16)
             last = t1 == T
-            weights = gate_banks[t0 // TOK][:, :, t0 % TOK : t0 % TOK + n]
+            lists = slice(t0 // 16, t1 // 16)
             total = keep.tile([P, PACK, n], F32, name=f"total{t0}")
-            rounded = keep.tile([P, n, PACK], BF16, name=f"rounded{t0}", align_bytes=64)
+            terms = keep.tile([P, PACK, 2, n], F32, name=f"terms{t0}")
             for t in range(PACK):
-                terms = ring.tile([P, 2, n], F32, name="terms", bufs=4)
-                for r, pos_sb in enumerate((pos1_sb, pos2_sb)):
-                    looked_up = y[t][:].indirect(pos_sb[:, lists])
-                    if r == 0 and (t % 2 == 0 or t0 == 0 and t == 1):
-                        nc.vector.tensor_copy(out=terms[:, r, :], in_=looked_up)
-                    else:
-                        nc.scalar.activation(out=terms[:, r, :], in_=looked_up, func=COPY)
-                nc.vector.tensor_tensor(out=terms[:], in0=terms[:], in1=weights, op=MULT)
-                adder = nc.vector if last and t >= 2 else nc.gpsimd
-                adder.tensor_tensor(out=total[:, t, :], in0=terms[:, 0, :], in1=terms[:, 1, :], op=ADD)
+                nc.scalar.activation(out=terms[:, t, 1, :], in_=y[t][:].indirect(pos2_sb[:, lists]), func=COPY)
+                if t >= 2:
+                    nc.vector.tensor_tensor(out=terms[:, t, 0, :], in0=y[t][:].indirect(pos1_sb[:, lists]), in1=gates[:, 0, t0:t1], op=MULT)
+                    nc.vector.tensor_tensor(out=terms[:, t, 1, :], in0=terms[:, t, 1, :], in1=gates[:, 1, t0:t1], op=MULT)
+                else:
+                    nc.scalar.activation(out=terms[:, t, 0, :], in_=y[t][:].indirect(pos1_sb[:, lists]), func=COPY)
+                    nc.vector.tensor_tensor(out=terms[:, t], in0=terms[:, t], in1=gates[:, :, t0:t1], op=MULT)
+                nc.vector.tensor_tensor(out=total[:, t, :], in0=terms[:, t, 0, :], in1=terms[:, t, 1, :], op=ADD)
                 nc.sync.dma_start(out=out_rows[:, t, t0:t1], in_=total[:, t, :])
-            if last:
-                nc.vector.tensor_copy(
-                    out=rounded[:].rearrange("p (c i) t -> p c t i", i=4), in_=total[:].rearrange("p t (c i) -> p c t i", i=4)
-                )
-            else:
-                nc.gpsimd.tensor_copy(out=rounded[:], in_=total[:].rearrange("p t c -> p c t"))
+            rounded = keep.tile([P, n, PACK], BF16, name=f"rounded{t0}", align_bytes=64)
+            split = 0 if last else n
+            for round_copy, part in ((nc.scalar.copy, slice(0, split)), (nc.vector.tensor_copy, slice(split, n))):
+                if part.start < part.stop:
+                    round_copy(
+                        out=rounded[:, part, :].rearrange("p (c i) t -> p c t i", i=4),
+                        in_=total[:, :, part].rearrange("p t (c i) -> p c t i", i=4),
+                    )
             nc.vector.quantize_mx(
                 out=out_codes[:, t0:t1].bitcast(FP8X4), scales=out_plane[:, t0:t1], in_=rounded[:].rearrange("p c t -> p (c t)")
             )

@@ -22,6 +22,7 @@ COPY = mybir.ActivationFunctionType.Copy
 P = 128
 PACK = 4
 TOK = 256
+SLOT_STEPS = ((0, 256), (256, 768), (768, 1024), (1024, 1280), (1280, 1536))
 TOKEN_CHUNKS = ((0, 512), (512, 768))
 
 
@@ -45,10 +46,8 @@ def tile_moe_sup_glu_sigmoid_kernel(
         first_codes = [keep.tile([P, 2 * H], U8, name=f"first_codes{m}", align_bytes=64) for m in range(2)]
         first_plane = [keep.tile([P, H], U8, name=f"first_plane{m}", align_bytes=64) for m in range(2)]
         w2_raw = [keep.tile([P, 2, 2 * N], U8, name=f"w2_raw{c}") for c in range(E // 2)]
-        w2_raw_plane = keep.tile([P, 2, N], U8, name="w2_raw_plane")
-        w2_dealt_plane = keep.tile([P, 2, N], U8, name="w2_dealt_plane", align_bytes=64)
-        w2_moved_plane = keep.tile([P, 4, N], U8, name="w2_moved_plane", align_bytes=64)
-        w2_plane = [w2_dealt_plane[:, e // 4, :] if e % 4 == 0 else w2_moved_plane[:, e - 1 - e // 4, :] for e in range(E)]
+        w2_raw_plane = keep.tile([P, E, N], U8, name="w2_raw_plane")
+        w2_plane = [keep.tile([P, N], U8, name=f"w2_plane{e}", align_bytes=64) for e in range(E)]
         gates = keep.tile([P, 2, T], F32, name="gates")
 
         def load_scale_rows(plane, rows, which):
@@ -71,7 +70,6 @@ def tile_moe_sup_glu_sigmoid_kernel(
         nc.gpsimd.memset(x_plane[:].bitcast(I32), 0)
         nc.gpsimd.memset(first_raw_plane[1][:].bitcast(I32), 0)
         nc.gpsimd.memset(w2_raw_plane[:].rearrange("p e n -> p (e n)").bitcast(I32), 0)
-        nc.gpsimd.memset(w2_moved_plane[:].rearrange("p e n -> p (e n)").bitcast(I32), 0)
 
         nc.sync.dma_start(out=first_raw[0][:].bitcast(I32), in_=w1_words[0].bitcast(I32))
         load_scale_rows(first_raw_plane[0], w1_scales[0], range(4))
@@ -81,12 +79,7 @@ def tile_moe_sup_glu_sigmoid_kernel(
         load_scale_rows(x_plane, x_scales[0], range(1, 4))
         load_scale_rows(first_raw_plane[1], w3_scales[0], range(4))
         nc.sync.dma_start(offs_sb[:], offs)
-        for g, (e0, e1) in enumerate(((0, 4), (4, E))):
-            for q in range(4):
-                nc.sync.dma_start(
-                    out=w2_raw_plane[32 * q : 32 * q + 4 * (e1 - e0), g, :].bitcast(I32),
-                    in_=w2_scales[e0:e1, 0, 4 * q : 4 * q + 4, :].bitcast(I32),
-                )
+        load_scale_rows(w2_raw_plane, w2_scales[:, 0].rearrange("e q n -> q e n"), range(4))
         for c in range(E // 2):
             nc.sync.dma_start(out=w2_raw[c][:].bitcast(I32), in_=w2_words[2 * c : 2 * c + 2, 0].rearrange("e p b -> p e b").bitcast(I32))
         nc.sync.dma_start(pos1_sb[:], pos1)
@@ -116,7 +109,7 @@ def tile_moe_sup_glu_sigmoid_kernel(
                             stop=True,
                         )
                     sums.append(bank)
-                sig = keep.tile([P, TOK, 2], F32, name="sig", tag=f"shared{t0}", align_bytes=64)
+                sig = keep.tile([P, TOK, 2], F32, name="sig", tag=f"shared{u}{t0}", align_bytes=64)
                 nc.scalar.activation(out=sig[:], in_=sums[0][:].rearrange("p j n -> p n j"), func=SIGMOID)
                 nc.vector.tensor_tensor(
                     out=h_pairs[u][:, cols].bitcast(BF16).rearrange("p (n j) -> p n j", j=2),
@@ -125,64 +118,65 @@ def tile_moe_sup_glu_sigmoid_kernel(
                     op=MULT,
                 )
 
-        w2_pairs = [keep.tile([P, 2, 2 * N], U8, name="w2_pair", tag=f"shared{t0}", align_bytes=64) for t0 in range(0, T, TOK)]
+        w2_pairs = [keep.tile([P, 2, 2 * N], U8, name="w2_pair", tag=f"shared1{t0}", align_bytes=64) for t0 in range(0, T, TOK)]
         w2_codes = [w2_pairs[e // 2][:, e % 2, :] for e in range(E)]
-        for g in range(2):
-            deal_bytes(nc.vector.tensor_copy, w2_dealt_plane[:, g, :], w2_raw_plane[:, g, :])
         for e in range(E):
-            if e % 4:
-                for r in range(4):
-                    nc.sync.dma_start(
-                        out=w2_plane[e][r:P:32].bitcast(I32), in_=w2_dealt_plane[4 * (e % 4) + r : P : 32, e // 4, :].bitcast(I32)
-                    )
+            deal_bytes(nc.gpsimd.tensor_copy, w2_plane[e][:], w2_raw_plane[:, e, :])
 
         y = [keep.tile([P, S], F32, name=f"y{t}") for t in range(PACK)]
         picked, woven = {}, {}
+        steps = len(SLOT_STEPS)
 
-        def pick(e, u):
+        def pick(s, u):
+            s0, s1 = SLOT_STEPS[s]
             if u == 0:
-                picked[e] = keep.tile([P, 2, C], U32, name="picked", tag=f"stage{e % 2}{e // 2 % 2}", align_bytes=64)
-            nc.vector.tensor_copy(out=picked[e][:, u, :], in_=h_pairs[u][:].indirect(offs_sb[:, e * C // 16 : (e + 1) * C // 16]))
+                picked[s] = keep.tile([P, 2, s1 - s0], U32, name="picked", tag=f"stage{s % 2}{s // 2 % 2}", align_bytes=64)
+            nc.vector.tensor_copy(out=picked[s][:, u, :], in_=h_pairs[u][:].indirect(offs_sb[:, s0 // 16 : s1 // 16]))
 
-        def weave(e):
-            woven[e] = keep.tile([P, C, 2], U32, name="woven", tag=f"stage{e % 2}{1 - e // 2 % 2}", align_bytes=64)
+        def weave(s):
+            s0, s1 = SLOT_STEPS[s]
+            woven[s] = keep.tile([P, s1 - s0, 2], U32, name="woven", tag=f"stage{s % 2}{1 - s // 2 % 2}", align_bytes=64)
             if False:
-                nc.scalar.copy(out=woven[e][:], in_=picked[e][:].rearrange("p u n -> p n u"))
+                nc.vector.tensor_copy(out=woven[s][:].bitcast(I32), in_=picked[s][:].bitcast(I32).rearrange("p u n -> p n u"))
             else:
-                nc.vector.tensor_copy(out=woven[e][:].bitcast(I32), in_=picked[e][:].bitcast(I32).rearrange("p u n -> p n u"))
+                nc.gpsimd.tensor_copy(out=woven[s][:], in_=picked[s][:].rearrange("p u n -> p n u"))
 
-        def expert(e):
-            deal_words(nc.scalar.copy, w2_codes[e], w2_raw[e // 2][:, e % 2, :])
-            h_codes = ring.tile([P, C], U32, name="h_codes", align_bytes=64)
-            h_plane = ring.tile([P, C], U8, name="h_plane", align_bytes=64)
+        def multiply(s):
+            s0, s1 = SLOT_STEPS[s]
+            h_codes = ring.tile([P, s1 - s0], U32, name="h_codes", align_bytes=64)
+            h_plane = ring.tile([P, s1 - s0], U8, name="h_plane", align_bytes=64)
             nc.vector.quantize_mx(
-                out=h_codes[:].bitcast(FP8X4), scales=h_plane[:], in_=woven[e][:].rearrange("p n u -> p (n u)").bitcast(BF16)
+                out=h_codes[:].bitcast(FP8X4), scales=h_plane[:], in_=woven[s][:].rearrange("p n u -> p (n u)").bitcast(BF16)
             )
             for t in range(PACK):
-                bank = psum.tile([P, C], F32, name="bank", tag="bank")
-                nc.tensor.matmul_mx(
-                    out=bank[:],
-                    lhsT=w2_codes[e][:, 2 * P * t : 2 * P * (t + 1)].bitcast(FP4X4),
-                    lhsT_scale=w2_plane[e][:, P * t : P * (t + 1)],
-                    rhs=h_codes[:].bitcast(FP8X4),
-                    rhs_scale=h_plane[:],
-                    start=True,
-                    stop=True,
-                )
-                if e == E - 1 and t >= 2:
-                    nc.vector.tensor_copy(out=y[t][:, e * C : (e + 1) * C], in_=bank[:])
+                bank = psum.tile([P, s1 - s0], F32, name="bank", tag="bank")
+                for c0 in range(s0, s1, C):
+                    e, c1 = c0 // C, min(s1, c0 + C)
+                    nc.tensor.matmul_mx(
+                        out=bank[:, c0 - s0 : c1 - s0],
+                        lhsT=w2_codes[e][:, 2 * P * t : 2 * P * (t + 1)].bitcast(FP4X4),
+                        lhsT_scale=w2_plane[e][:, P * t : P * (t + 1)],
+                        rhs=h_codes[:, c0 - s0 : c1 - s0].bitcast(FP8X4),
+                        rhs_scale=h_plane[:, c0 - s0 : c1 - s0],
+                        start=True,
+                        stop=True,
+                    )
+                if s == steps - 1 and t < 2:
+                    nc.vector.tensor_copy(out=y[t][:, s0:s1], in_=bank[:])
                 else:
-                    nc.scalar.copy(out=y[t][:, e * C : (e + 1) * C], in_=bank[:])
+                    nc.scalar.copy(out=y[t][:, s0:s1], in_=bank[:])
 
+        for e in range(E):
+            deal_words(nc.scalar.copy, w2_codes[e], w2_raw[e // 2][:, e % 2, :])
         pick(0, 0)
         pick(0, 1)
-        for e in range(E):
-            if e + 1 < E:
-                pick(e + 1, 0)
-            weave(e)
-            if e + 1 < E:
-                pick(e + 1, 1)
-            expert(e)
+        for s in range(steps):
+            if s + 1 < steps:
+                pick(s + 1, 0)
+            weave(s)
+            if s + 1 < steps:
+                pick(s + 1, 1)
+            multiply(s)
 
         out_codes = keep.tile([P, T], U32, name="out_codes", align_bytes=64)
         out_plane = keep.tile([P, T], U8, name="out_plane", align_bytes=64)
@@ -195,7 +189,7 @@ def tile_moe_sup_glu_sigmoid_kernel(
             terms = keep.tile([P, PACK, 2, n], F32, name=f"terms{t0}")
             for t in range(PACK):
                 nc.scalar.activation(out=terms[:, t, 1, :], in_=y[t][:].indirect(pos2_sb[:, lists]), func=COPY)
-                if t >= 2:
+                if t < 3:
                     nc.vector.tensor_tensor(out=terms[:, t, 0, :], in0=y[t][:].indirect(pos1_sb[:, lists]), in1=gates[:, 0, t0:t1], op=MULT)
                     nc.vector.tensor_tensor(out=terms[:, t, 1, :], in0=terms[:, t, 1, :], in1=gates[:, 1, t0:t1], op=MULT)
                 else:
@@ -204,7 +198,7 @@ def tile_moe_sup_glu_sigmoid_kernel(
                 nc.vector.tensor_tensor(out=total[:, t, :], in0=terms[:, t, 0, :], in1=terms[:, t, 1, :], op=ADD)
                 nc.sync.dma_start(out=out_rows[:, t, t0:t1], in_=total[:, t, :])
             rounded = keep.tile([P, n, PACK], BF16, name=f"rounded{t0}", align_bytes=64)
-            split = 0 if last else n
+            split = 96 if last else n
             for round_copy, part in ((nc.scalar.copy, slice(0, split)), (nc.vector.tensor_copy, slice(split, n))):
                 if part.start < part.stop:
                     round_copy(

@@ -3,8 +3,8 @@ from contextlib import ExitStack
 import concourse.mybir as mybir
 
 K, T, E, C, H, N = 512, 768, 6, 256, 512, 512
-S = E * C
-FLOPS = 2 * K * H * T * 2 + 2 * H * N * S
+SLOTS = E * C
+FLOPS = 2 * (2 * K * H * T) + 2 * H * N * SLOTS
 
 F32 = mybir.dt.float32
 BF16 = mybir.dt.bfloat16
@@ -21,9 +21,14 @@ COPY = mybir.ActivationFunctionType.Copy
 
 P = 128
 PACK = 4
-TOK = 256
+QUADRANT = 32
+LIST_ROWS = 16
+TOKEN_BLOCK = 256
 SLOT_STEPS = ((0, 256), (256, 768), (768, 1024), (1024, 1280), (1280, 1536))
-TOKEN_CHUNKS = ((0, 512), (512, 768))
+TOKEN_STEPS = ((0, 512), (512, 768))
+VECTOR_LOOKUP_SETS = 3
+VECTOR_EMPTIED_SETS = 2
+SCALAR_ROUNDED_LAST = 96
 
 
 def tile_moe_sup_glu_sigmoid_kernel(
@@ -35,24 +40,24 @@ def tile_moe_sup_glu_sigmoid_kernel(
         ring = ctx.enter_context(tc.tile_pool(name="ring", bufs=2))
         psum = ctx.enter_context(tc.psum_pool(name="psum", bufs=8))
 
-        offs_sb = keep.tile([P, S // 16], U16, name="offs_sb")
-        pos1_sb = keep.tile([P, T // 16], U16, name="pos1_sb")
-        pos2_sb = keep.tile([P, T // 16], U16, name="pos2_sb")
+        offs_sb = keep.tile([P, SLOTS // LIST_ROWS], U16, name="offs_sb")
+        pos1_sb = keep.tile([P, T // LIST_ROWS], U16, name="pos1_sb")
+        pos2_sb = keep.tile([P, T // LIST_ROWS], U16, name="pos2_sb")
 
         x_codes = keep.tile([P, T], U32, name="x_codes", align_bytes=64)
-        x_plane = keep.tile([P, T], U8, name="x_plane", align_bytes=64)
-        first_raw = [keep.tile([P, 2 * H], U8, name=f"first_raw{m}") for m in range(2)]
-        first_raw_plane = [keep.tile([P, H], U8, name=f"first_raw_plane{m}") for m in range(2)]
+        x_scale_tile = keep.tile([P, T], U8, name="x_scale_tile", align_bytes=64)
+        first_loaded = [keep.tile([P, 2 * H], U8, name=f"first_loaded{m}") for m in range(2)]
+        first_loaded_scales = [keep.tile([P, H], U8, name=f"first_loaded_scales{m}") for m in range(2)]
         first_codes = [keep.tile([P, 2 * H], U8, name=f"first_codes{m}", align_bytes=64) for m in range(2)]
-        first_plane = [keep.tile([P, H], U8, name=f"first_plane{m}", align_bytes=64) for m in range(2)]
-        w2_raw = [keep.tile([P, 2, 2 * N], U8, name=f"w2_raw{c}") for c in range(E // 2)]
-        w2_raw_plane = keep.tile([P, E, N], U8, name="w2_raw_plane")
-        w2_plane = [keep.tile([P, N], U8, name=f"w2_plane{e}", align_bytes=64) for e in range(E)]
+        first_scale_tile = [keep.tile([P, H], U8, name=f"first_scale_tile{m}", align_bytes=64) for m in range(2)]
+        w2_loaded = [keep.tile([P, 2, 2 * N], U8, name=f"w2_loaded{pair}") for pair in range(E // 2)]
+        w2_loaded_scales = keep.tile([P, E, N], U8, name="w2_loaded_scales")
+        w2_scale_tile = [keep.tile([P, N], U8, name=f"w2_scale_tile{e}", align_bytes=64) for e in range(E)]
         gates = keep.tile([P, 2, T], F32, name="gates")
 
-        def load_scale_rows(plane, rows, which):
+        def load_scale_rows(scale_tile, rows, which):
             for r in which:
-                nc.sync.dma_start(out=plane[r:P:32].bitcast(I32), in_=rows[r:16:4].bitcast(I32))
+                nc.sync.dma_start(out=scale_tile[r:P:QUADRANT].bitcast(I32), in_=rows[r:16:4].bitcast(I32))
 
         def deal_words(engine_copy, dst, src):
             engine_copy(
@@ -66,50 +71,52 @@ def tile_moe_sup_glu_sigmoid_kernel(
                 in_=src.rearrange("p (b i t) -> p b t i", t=PACK, i=16),
             )
 
-        nc.gpsimd.memset(first_raw_plane[0][:].bitcast(I32), 0)
-        nc.gpsimd.memset(x_plane[:].bitcast(I32), 0)
-        nc.gpsimd.memset(first_raw_plane[1][:].bitcast(I32), 0)
-        nc.gpsimd.memset(w2_raw_plane[:].rearrange("p e n -> p (e n)").bitcast(I32), 0)
+        nc.gpsimd.memset(first_loaded_scales[0][:].bitcast(I32), 0)
+        nc.gpsimd.memset(x_scale_tile[:].bitcast(I32), 0)
+        nc.gpsimd.memset(first_loaded_scales[1][:].bitcast(I32), 0)
+        nc.gpsimd.memset(w2_loaded_scales[:].rearrange("p e n -> p (e n)").bitcast(I32), 0)
 
-        nc.sync.dma_start(out=first_raw[0][:].bitcast(I32), in_=w1_words[0].bitcast(I32))
-        load_scale_rows(first_raw_plane[0], w1_scales[0], range(4))
-        nc.sync.dma_start(out=first_raw[1][:].bitcast(I32), in_=w3_words[0].bitcast(I32))
-        load_scale_rows(x_plane, x_scales[0], range(1))
+        nc.sync.dma_start(out=first_loaded[0][:].bitcast(I32), in_=w1_words[0].bitcast(I32))
+        load_scale_rows(first_loaded_scales[0], w1_scales[0], range(4))
+        nc.sync.dma_start(out=first_loaded[1][:].bitcast(I32), in_=w3_words[0].bitcast(I32))
+        load_scale_rows(x_scale_tile, x_scales[0], range(1))
         nc.sync.dma_start(out=x_codes[:].bitcast(I32), in_=x_words[0].rearrange("p n t -> p (n t)").bitcast(I32))
-        load_scale_rows(x_plane, x_scales[0], range(1, 4))
-        load_scale_rows(first_raw_plane[1], w3_scales[0], range(4))
+        load_scale_rows(x_scale_tile, x_scales[0], range(1, 4))
+        load_scale_rows(first_loaded_scales[1], w3_scales[0], range(4))
         nc.sync.dma_start(offs_sb[:], offs)
-        load_scale_rows(w2_raw_plane, w2_scales[:, 0].rearrange("e q n -> q e n"), range(4))
-        for c in range(E // 2):
-            nc.sync.dma_start(out=w2_raw[c][:].bitcast(I32), in_=w2_words[2 * c : 2 * c + 2, 0].rearrange("e p b -> p e b").bitcast(I32))
+        load_scale_rows(w2_loaded_scales, w2_scales[:, 0].rearrange("e q n -> q e n"), range(4))
+        for pair in range(E // 2):
+            nc.sync.dma_start(
+                out=w2_loaded[pair][:].bitcast(I32), in_=w2_words[2 * pair : 2 * pair + 2, 0].rearrange("e p b -> p e b").bitcast(I32)
+            )
         nc.sync.dma_start(pos1_sb[:], pos1)
         nc.sync.dma_start(pos2_sb[:], pos2)
         nc.sync.dma_start(out=gates[:], in_=gate.rearrange("r p c -> p r c"))
 
         for m in range(2):
-            deal_words(nc.vector.tensor_copy, first_codes[m][:], first_raw[m][:])
-            deal_bytes(nc.vector.tensor_copy, first_plane[m][:], first_raw_plane[m][:])
+            deal_words(nc.vector.tensor_copy, first_codes[m][:], first_loaded[m][:])
+            deal_bytes(nc.vector.tensor_copy, first_scale_tile[m][:], first_loaded_scales[m][:])
 
         h_pairs = [keep.tile([P, T], U32, name=f"h_pairs{u}") for u in range(2)]
         for u in range(2):
-            for t0 in range(0, T, TOK):
-                cols = slice(t0, t0 + TOK)
+            for t0 in range(0, T, TOKEN_BLOCK):
+                cols = slice(t0, t0 + TOKEN_BLOCK)
                 sums = []
                 for m in range(2):
-                    bank = psum.tile([P, 2, TOK], F32, name="bank", tag="bank")
+                    bank = psum.tile([P, 2, TOKEN_BLOCK], F32, name="bank", tag="bank")
                     for j in range(2):
                         t = 2 * u + j
                         nc.tensor.matmul_mx(
                             out=bank[:, j, :],
                             lhsT=first_codes[m][:, 2 * P * t : 2 * P * (t + 1)].bitcast(FP4X4),
-                            lhsT_scale=first_plane[m][:, P * t : P * (t + 1)],
+                            lhsT_scale=first_scale_tile[m][:, P * t : P * (t + 1)],
                             rhs=x_codes[:, cols].bitcast(FP8X4),
-                            rhs_scale=x_plane[:, cols],
+                            rhs_scale=x_scale_tile[:, cols],
                             start=True,
                             stop=True,
                         )
                     sums.append(bank)
-                sig = keep.tile([P, TOK, 2], F32, name="sig", tag=f"shared{u}{t0}", align_bytes=64)
+                sig = keep.tile([P, TOKEN_BLOCK, 2], F32, name="sig", tag=f"shared{u}{t0}", align_bytes=64)
                 nc.scalar.activation(out=sig[:], in_=sums[0][:].rearrange("p j n -> p n j"), func=SIGMOID)
                 nc.vector.tensor_tensor(
                     out=h_pairs[u][:, cols].bitcast(BF16).rearrange("p (n j) -> p n j", j=2),
@@ -118,56 +125,54 @@ def tile_moe_sup_glu_sigmoid_kernel(
                     op=MULT,
                 )
 
-        w2_pairs = [keep.tile([P, 2, 2 * N], U8, name="w2_pair", tag=f"shared1{t0}", align_bytes=64) for t0 in range(0, T, TOK)]
+        w2_pairs = [keep.tile([P, 2, 2 * N], U8, name="w2_pair", tag=f"shared1{t0}", align_bytes=64) for t0 in range(0, T, TOKEN_BLOCK)]
         w2_codes = [w2_pairs[e // 2][:, e % 2, :] for e in range(E)]
         for e in range(E):
-            deal_bytes(nc.gpsimd.tensor_copy, w2_plane[e][:], w2_raw_plane[:, e, :])
+            deal_bytes(nc.gpsimd.tensor_copy, w2_scale_tile[e][:], w2_loaded_scales[:, e, :])
 
-        y = [keep.tile([P, S], F32, name=f"y{t}") for t in range(PACK)]
+        y = [keep.tile([P, SLOTS], F32, name=f"y{t}") for t in range(PACK)]
         picked, woven = {}, {}
         steps = len(SLOT_STEPS)
 
         def pick(s, u):
             s0, s1 = SLOT_STEPS[s]
             if u == 0:
-                picked[s] = keep.tile([P, 2, s1 - s0], U32, name="picked", tag=f"stage{s % 2}{s // 2 % 2}", align_bytes=64)
-            nc.vector.tensor_copy(out=picked[s][:, u, :], in_=h_pairs[u][:].indirect(offs_sb[:, s0 // 16 : s1 // 16]))
+                picked[s] = ring.tile([P, 2, s1 - s0], U32, name="picked")
+            nc.vector.tensor_copy(out=picked[s][:, u, :], in_=h_pairs[u][:].indirect(offs_sb[:, s0 // LIST_ROWS : s1 // LIST_ROWS]))
 
         def weave(s):
             s0, s1 = SLOT_STEPS[s]
-            woven[s] = keep.tile([P, s1 - s0, 2], U32, name="woven", tag=f"stage{s % 2}{1 - s // 2 % 2}", align_bytes=64)
-            if False:
-                nc.vector.tensor_copy(out=woven[s][:].bitcast(I32), in_=picked[s][:].bitcast(I32).rearrange("p u n -> p n u"))
-            else:
-                nc.gpsimd.tensor_copy(out=woven[s][:], in_=picked[s][:].rearrange("p u n -> p n u"))
+            woven[s] = ring.tile([P, s1 - s0, 2], U32, name="woven", align_bytes=64)
+            nc.gpsimd.tensor_copy(out=woven[s][:], in_=picked[s][:].rearrange("p u n -> p n u"))
 
         def multiply(s):
             s0, s1 = SLOT_STEPS[s]
             h_codes = ring.tile([P, s1 - s0], U32, name="h_codes", align_bytes=64)
-            h_plane = ring.tile([P, s1 - s0], U8, name="h_plane", align_bytes=64)
+            h_scale_tile = ring.tile([P, s1 - s0], U8, name="h_scale_tile", align_bytes=64)
             nc.vector.quantize_mx(
-                out=h_codes[:].bitcast(FP8X4), scales=h_plane[:], in_=woven[s][:].rearrange("p n u -> p (n u)").bitcast(BF16)
+                out=h_codes[:].bitcast(FP8X4), scales=h_scale_tile[:], in_=woven[s][:].rearrange("p n u -> p (n u)").bitcast(BF16)
             )
             for t in range(PACK):
                 bank = psum.tile([P, s1 - s0], F32, name="bank", tag="bank")
                 for c0 in range(s0, s1, C):
-                    e, c1 = c0 // C, min(s1, c0 + C)
+                    e = c0 // C
+                    cols = slice(c0 - s0, c0 - s0 + C)
                     nc.tensor.matmul_mx(
-                        out=bank[:, c0 - s0 : c1 - s0],
+                        out=bank[:, cols],
                         lhsT=w2_codes[e][:, 2 * P * t : 2 * P * (t + 1)].bitcast(FP4X4),
-                        lhsT_scale=w2_plane[e][:, P * t : P * (t + 1)],
-                        rhs=h_codes[:, c0 - s0 : c1 - s0].bitcast(FP8X4),
-                        rhs_scale=h_plane[:, c0 - s0 : c1 - s0],
+                        lhsT_scale=w2_scale_tile[e][:, P * t : P * (t + 1)],
+                        rhs=h_codes[:, cols].bitcast(FP8X4),
+                        rhs_scale=h_scale_tile[:, cols],
                         start=True,
                         stop=True,
                     )
-                if s == steps - 1 and t < 2:
+                if s == steps - 1 and t < VECTOR_EMPTIED_SETS:
                     nc.vector.tensor_copy(out=y[t][:, s0:s1], in_=bank[:])
                 else:
                     nc.scalar.copy(out=y[t][:, s0:s1], in_=bank[:])
 
         for e in range(E):
-            deal_words(nc.scalar.copy, w2_codes[e], w2_raw[e // 2][:, e % 2, :])
+            deal_words(nc.scalar.copy, w2_codes[e], w2_loaded[e // 2][:, e % 2, :])
         pick(0, 0)
         pick(0, 1)
         for s in range(steps):
@@ -179,17 +184,16 @@ def tile_moe_sup_glu_sigmoid_kernel(
             multiply(s)
 
         out_codes = keep.tile([P, T], U32, name="out_codes", align_bytes=64)
-        out_plane = keep.tile([P, T], U8, name="out_plane", align_bytes=64)
+        out_scale_tile = keep.tile([P, T], U8, name="out_scale_tile", align_bytes=64)
         out_rows = out_0.rearrange("(p t) c -> p t c", t=PACK)
-        for c, (t0, t1) in enumerate(TOKEN_CHUNKS):
-            n = t1 - t0
-            last = t1 == T
-            lists = slice(t0 // 16, t1 // 16)
-            total = keep.tile([P, PACK, n], F32, name=f"total{t0}")
-            terms = keep.tile([P, PACK, 2, n], F32, name=f"terms{t0}")
+        for t0, t1 in TOKEN_STEPS:
+            tokens = t1 - t0
+            lists = slice(t0 // LIST_ROWS, t1 // LIST_ROWS)
+            total = keep.tile([P, PACK, tokens], F32, name=f"total{t0}")
+            terms = keep.tile([P, PACK, 2, tokens], F32, name=f"terms{t0}")
             for t in range(PACK):
                 nc.scalar.activation(out=terms[:, t, 1, :], in_=y[t][:].indirect(pos2_sb[:, lists]), func=COPY)
-                if t < 3:
+                if t < VECTOR_LOOKUP_SETS:
                     nc.vector.tensor_tensor(out=terms[:, t, 0, :], in0=y[t][:].indirect(pos1_sb[:, lists]), in1=gates[:, 0, t0:t1], op=MULT)
                     nc.vector.tensor_tensor(out=terms[:, t, 1, :], in0=terms[:, t, 1, :], in1=gates[:, 1, t0:t1], op=MULT)
                 else:
@@ -197,20 +201,23 @@ def tile_moe_sup_glu_sigmoid_kernel(
                     nc.vector.tensor_tensor(out=terms[:, t], in0=terms[:, t], in1=gates[:, :, t0:t1], op=MULT)
                 nc.vector.tensor_tensor(out=total[:, t, :], in0=terms[:, t, 0, :], in1=terms[:, t, 1, :], op=ADD)
                 nc.sync.dma_start(out=out_rows[:, t, t0:t1], in_=total[:, t, :])
-            rounded = keep.tile([P, n, PACK], BF16, name=f"rounded{t0}", align_bytes=64)
-            split = 96 if last else n
-            for round_copy, part in ((nc.scalar.copy, slice(0, split)), (nc.vector.tensor_copy, slice(split, n))):
-                if part.start < part.stop:
-                    round_copy(
-                        out=rounded[:, part, :].rearrange("p (c i) t -> p c t i", i=4),
-                        in_=total[:, :, part].rearrange("p t (c i) -> p c t i", i=4),
-                    )
+            rounded = keep.tile([P, tokens, PACK], BF16, name=f"rounded{t0}", align_bytes=64)
+            split = SCALAR_ROUNDED_LAST if t1 == T else tokens
+            nc.scalar.copy(
+                out=rounded[:, :split, :].rearrange("p (c i) t -> p c t i", i=4),
+                in_=total[:, :, :split].rearrange("p t (c i) -> p c t i", i=4),
+            )
+            if split < tokens:
+                nc.vector.tensor_copy(
+                    out=rounded[:, split:, :].rearrange("p (c i) t -> p c t i", i=4),
+                    in_=total[:, :, split:].rearrange("p t (c i) -> p c t i", i=4),
+                )
             nc.vector.quantize_mx(
-                out=out_codes[:, t0:t1].bitcast(FP8X4), scales=out_plane[:, t0:t1], in_=rounded[:].rearrange("p c t -> p (c t)")
+                out=out_codes[:, t0:t1].bitcast(FP8X4), scales=out_scale_tile[:, t0:t1], in_=rounded[:].rearrange("p c t -> p (c t)")
             )
             nc.sync.dma_start(
                 out=out_1[0, :, t0:t1, :].rearrange("p c d -> p (c d)").bitcast(I32), in_=out_codes[:, t0:t1].bitcast(I32)
             )
         for r in range(4):
             queue = nc.sync if r % 2 == 0 else nc.scalar
-            queue.dma_start(out=out_2[0, r:16:4].bitcast(I32), in_=out_plane[r:P:32].bitcast(I32))
+            queue.dma_start(out=out_2[0, r:16:4].bitcast(I32), in_=out_scale_tile[r:P:QUADRANT].bitcast(I32))

from contextlib import ExitStack

import concourse.mybir as mybir

K, T, E, C, H, N = 512, 768, 6, 256, 512, 512
SLOTS = E * C
FLOPS = 2 * (2 * K * H * T) + 2 * H * N * SLOTS

F32 = mybir.dt.float32
BF16 = mybir.dt.bfloat16
I32 = mybir.dt.int32
U32 = mybir.dt.uint32
U16 = mybir.dt.uint16
U8 = mybir.dt.uint8
FP8X4 = mybir.dt.float8_e4m3fn_x4
FP4X4 = mybir.dt.float4_e2m1fn_x4
MULT = mybir.AluOpType.mult
ADD = mybir.AluOpType.add
SIGMOID = mybir.ActivationFunctionType.Sigmoid
COPY = mybir.ActivationFunctionType.Copy

P = 128
PACK = 4
QUADRANT = 32
LIST_ROWS = 16
TOKEN_BLOCK = 256
SLOT_STEPS = ((0, 256), (256, 768), (768, 1024), (1024, 1280), (1280, 1536))
TOKEN_STEPS = ((0, 512), (512, 768))
VECTOR_LOOKUP_SETS = 3
VECTOR_EMPTIED_SETS = 2
SCALAR_ROUNDED_LAST = 96


def tile_moe_sup_glu_sigmoid_kernel(
    tc, x_words, x_scales, w1_words, w1_scales, w3_words, w3_scales, w2_words, w2_scales, gate, offs, pos1, pos2, out_0, out_1, out_2
):
    nc = tc.nc
    with ExitStack() as ctx:
        keep = ctx.enter_context(tc.tile_pool(name="keep", bufs=1))
        ring = ctx.enter_context(tc.tile_pool(name="ring", bufs=2))
        psum = ctx.enter_context(tc.psum_pool(name="psum", bufs=8))

        offs_sb = keep.tile([P, SLOTS // LIST_ROWS], U16, name="offs_sb")
        pos1_sb = keep.tile([P, T // LIST_ROWS], U16, name="pos1_sb")
        pos2_sb = keep.tile([P, T // LIST_ROWS], U16, name="pos2_sb")

        x_codes = keep.tile([P, T], U32, name="x_codes", align_bytes=64)
        x_scale_tile = keep.tile([P, T], U8, name="x_scale_tile", align_bytes=64)
        first_loaded = [keep.tile([P, 2 * H], U8, name=f"first_loaded{m}") for m in range(2)]
        first_loaded_scales = [keep.tile([P, H], U8, name=f"first_loaded_scales{m}") for m in range(2)]
        first_codes = [keep.tile([P, 2 * H], U8, name=f"first_codes{m}", align_bytes=64) for m in range(2)]
        first_scale_tile = [keep.tile([P, H], U8, name=f"first_scale_tile{m}", align_bytes=64) for m in range(2)]
        w2_loaded = [keep.tile([P, 2, 2 * N], U8, name=f"w2_loaded{pair}") for pair in range(E // 2)]
        w2_loaded_scales = keep.tile([P, E, N], U8, name="w2_loaded_scales")
        w2_scale_tile = [keep.tile([P, N], U8, name=f"w2_scale_tile{e}", align_bytes=64) for e in range(E)]
        gates = keep.tile([P, 2, T], F32, name="gates")

        def load_scale_rows(scale_tile, rows, which):
            for r in which:
                nc.sync.dma_start(out=scale_tile[r:P:QUADRANT].bitcast(I32), in_=rows[r:16:4].bitcast(I32))

        def deal_words(engine_copy, dst, src):
            engine_copy(
                out=dst.bitcast(U16).rearrange("p (t b i) -> p b t i", t=PACK, i=8),
                in_=src.bitcast(U16).rearrange("p (b i t) -> p b t i", t=PACK, i=8),
            )

        def deal_bytes(engine_copy, dst, src):
            engine_copy(
                out=dst.rearrange("p (t b i) -> p b t i", t=PACK, i=16),
                in_=src.rearrange("p (b i t) -> p b t i", t=PACK, i=16),
            )

        nc.gpsimd.memset(first_loaded_scales[0][:].bitcast(I32), 0)
        nc.gpsimd.memset(x_scale_tile[:].bitcast(I32), 0)
        nc.gpsimd.memset(first_loaded_scales[1][:].bitcast(I32), 0)
        nc.gpsimd.memset(w2_loaded_scales[:].rearrange("p e n -> p (e n)").bitcast(I32), 0)

        nc.sync.dma_start(out=first_loaded[0][:].bitcast(I32), in_=w1_words[0].bitcast(I32))
        load_scale_rows(first_loaded_scales[0], w1_scales[0], range(4))
        nc.sync.dma_start(out=first_loaded[1][:].bitcast(I32), in_=w3_words[0].bitcast(I32))
        load_scale_rows(x_scale_tile, x_scales[0], range(1))
        nc.sync.dma_start(out=x_codes[:].bitcast(I32), in_=x_words[0].rearrange("p n t -> p (n t)").bitcast(I32))
        load_scale_rows(x_scale_tile, x_scales[0], range(1, 4))
        load_scale_rows(first_loaded_scales[1], w3_scales[0], range(4))
        nc.sync.dma_start(offs_sb[:], offs)
        load_scale_rows(w2_loaded_scales, w2_scales[:, 0].rearrange("e q n -> q e n"), range(4))
        for pair in range(E // 2):
            nc.sync.dma_start(
                out=w2_loaded[pair][:].bitcast(I32), in_=w2_words[2 * pair : 2 * pair + 2, 0].rearrange("e p b -> p e b").bitcast(I32)
            )
        nc.sync.dma_start(pos1_sb[:], pos1)
        nc.sync.dma_start(pos2_sb[:], pos2)
        nc.sync.dma_start(out=gates[:], in_=gate.rearrange("r p c -> p r c"))

        for m in range(2):
            deal_words(nc.vector.tensor_copy, first_codes[m][:], first_loaded[m][:])
            deal_bytes(nc.vector.tensor_copy, first_scale_tile[m][:], first_loaded_scales[m][:])

        h_pairs = [keep.tile([P, T], U32, name=f"h_pairs{u}") for u in range(2)]
        for u in range(2):
            for t0 in range(0, T, TOKEN_BLOCK):
                cols = slice(t0, t0 + TOKEN_BLOCK)
                sums = []
                for m in range(2):
                    bank = psum.tile([P, 2, TOKEN_BLOCK], F32, name="bank", tag="bank")
                    for j in range(2):
                        t = 2 * u + j
                        nc.tensor.matmul_mx(
                            out=bank[:, j, :],
                            lhsT=first_codes[m][:, 2 * P * t : 2 * P * (t + 1)].bitcast(FP4X4),
                            lhsT_scale=first_scale_tile[m][:, P * t : P * (t + 1)],
                            rhs=x_codes[:, cols].bitcast(FP8X4),
                            rhs_scale=x_scale_tile[:, cols],
                            start=True,
                            stop=True,
                        )
                    sums.append(bank)
                sig = keep.tile([P, TOKEN_BLOCK, 2], F32, name="sig", tag=f"shared{u}{t0}", align_bytes=64)
                nc.scalar.activation(out=sig[:], in_=sums[0][:].rearrange("p j n -> p n j"), func=SIGMOID)
                nc.vector.tensor_tensor(
                    out=h_pairs[u][:, cols].bitcast(BF16).rearrange("p (n j) -> p n j", j=2),
                    in0=sums[1][:].rearrange("p j n -> p n j"),
                    in1=sig[:],
                    op=MULT,
                )

        w2_pairs = [keep.tile([P, 2, 2 * N], U8, name="w2_pair", tag=f"shared1{t0}", align_bytes=64) for t0 in range(0, T, TOKEN_BLOCK)]
        w2_codes = [w2_pairs[e // 2][:, e % 2, :] for e in range(E)]
        for e in range(E):
            deal_bytes(nc.gpsimd.tensor_copy, w2_scale_tile[e][:], w2_loaded_scales[:, e, :])

        y = [keep.tile([P, SLOTS], F32, name=f"y{t}") for t in range(PACK)]
        picked, woven = {}, {}
        steps = len(SLOT_STEPS)

        def pick(s, u):
            s0, s1 = SLOT_STEPS[s]
            if u == 0:
                picked[s] = ring.tile([P, 2, s1 - s0], U32, name="picked")
            nc.vector.tensor_copy(out=picked[s][:, u, :], in_=h_pairs[u][:].indirect(offs_sb[:, s0 // LIST_ROWS : s1 // LIST_ROWS]))

        def weave(s):
            s0, s1 = SLOT_STEPS[s]
            woven[s] = ring.tile([P, s1 - s0, 2], U32, name="woven", align_bytes=64)
            nc.gpsimd.tensor_copy(out=woven[s][:], in_=picked[s][:].rearrange("p u n -> p n u"))

        def multiply(s):
            s0, s1 = SLOT_STEPS[s]
            h_codes = ring.tile([P, s1 - s0], U32, name="h_codes", align_bytes=64)
            h_scale_tile = ring.tile([P, s1 - s0], U8, name="h_scale_tile", align_bytes=64)
            nc.vector.quantize_mx(
                out=h_codes[:].bitcast(FP8X4), scales=h_scale_tile[:], in_=woven[s][:].rearrange("p n u -> p (n u)").bitcast(BF16)
            )
            for t in range(PACK):
                bank = psum.tile([P, s1 - s0], F32, name="bank", tag="bank")
                for c0 in range(s0, s1, C):
                    e = c0 // C
                    cols = slice(c0 - s0, c0 - s0 + C)
                    nc.tensor.matmul_mx(
                        out=bank[:, cols],
                        lhsT=w2_codes[e][:, 2 * P * t : 2 * P * (t + 1)].bitcast(FP4X4),
                        lhsT_scale=w2_scale_tile[e][:, P * t : P * (t + 1)],
                        rhs=h_codes[:, cols].bitcast(FP8X4),
                        rhs_scale=h_scale_tile[:, cols],
                        start=True,
                        stop=True,
                    )
                if s == steps - 1 and t < VECTOR_EMPTIED_SETS:
                    nc.vector.tensor_copy(out=y[t][:, s0:s1], in_=bank[:])
                else:
                    nc.scalar.copy(out=y[t][:, s0:s1], in_=bank[:])

        for e in range(E):
            deal_words(nc.scalar.copy, w2_codes[e], w2_loaded[e // 2][:, e % 2, :])
        pick(0, 0)
        pick(0, 1)
        for s in range(steps):
            if s + 1 < steps:
                pick(s + 1, 0)
            weave(s)
            if s + 1 < steps:
                pick(s + 1, 1)
            multiply(s)

        out_codes = keep.tile([P, T], U32, name="out_codes", align_bytes=64)
        out_scale_tile = keep.tile([P, T], U8, name="out_scale_tile", align_bytes=64)
        out_rows = out_0.rearrange("(p t) c -> p t c", t=PACK)
        for t0, t1 in TOKEN_STEPS:
            tokens = t1 - t0
            lists = slice(t0 // LIST_ROWS, t1 // LIST_ROWS)
            total = keep.tile([P, PACK, tokens], F32, name=f"total{t0}")
            terms = keep.tile([P, PACK, 2, tokens], F32, name=f"terms{t0}")
            for t in range(PACK):
                nc.scalar.activation(out=terms[:, t, 1, :], in_=y[t][:].indirect(pos2_sb[:, lists]), func=COPY)
                if t < VECTOR_LOOKUP_SETS:
                    nc.vector.tensor_tensor(out=terms[:, t, 0, :], in0=y[t][:].indirect(pos1_sb[:, lists]), in1=gates[:, 0, t0:t1], op=MULT)
                    nc.vector.tensor_tensor(out=terms[:, t, 1, :], in0=terms[:, t, 1, :], in1=gates[:, 1, t0:t1], op=MULT)
                else:
                    nc.scalar.activation(out=terms[:, t, 0, :], in_=y[t][:].indirect(pos1_sb[:, lists]), func=COPY)
                    nc.vector.tensor_tensor(out=terms[:, t], in0=terms[:, t], in1=gates[:, :, t0:t1], op=MULT)
                nc.vector.tensor_tensor(out=total[:, t, :], in0=terms[:, t, 0, :], in1=terms[:, t, 1, :], op=ADD)
                nc.sync.dma_start(out=out_rows[:, t, t0:t1], in_=total[:, t, :])
            rounded = keep.tile([P, tokens, PACK], BF16, name=f"rounded{t0}", align_bytes=64)
            split = SCALAR_ROUNDED_LAST if t1 == T else tokens
            nc.scalar.copy(
                out=rounded[:, :split, :].rearrange("p (c i) t -> p c t i", i=4),
                in_=total[:, :, :split].rearrange("p t (c i) -> p c t i", i=4),
            )
            if split < tokens:
                nc.vector.tensor_copy(
                    out=rounded[:, split:, :].rearrange("p (c i) t -> p c t i", i=4),
                    in_=total[:, :, split:].rearrange("p t (c i) -> p c t i", i=4),
                )
            nc.vector.quantize_mx(
                out=out_codes[:, t0:t1].bitcast(FP8X4), scales=out_scale_tile[:, t0:t1], in_=rounded[:].rearrange("p c t -> p (c t)")
            )
            nc.sync.dma_start(
                out=out_1[0, :, t0:t1, :].rearrange("p c d -> p (c d)").bitcast(I32), in_=out_codes[:, t0:t1].bitcast(I32)
            )
        for r in range(4):
            queue = nc.sync if r % 2 == 0 else nc.scalar
            queue.dma_start(out=out_2[0, r:16:4].bitcast(I32), in_=out_scale_tile[r:P:QUADRANT].bitcast(I32))
